import numpy as np, ml_dtypes
CORES = [36,164,52,180,100,228,116,244]
N = 8
import mx_ref
BF = ml_dtypes.bfloat16
def entries(a):
    return np.ascontiguousarray(a.T).reshape(-1)
def table(e):
    return np.ascontiguousarray(np.reshape(e, (-1, 16)).T).astype(np.int32)
def f(rng, *shape):
    return mx_ref.flush((rng.standard_normal(shape, dtype=np.float32) * np.exp2(rng.integers(-2, 3, shape[:-1] + (1,)))).astype(BF))
def wide(rng, *shape, cols=0):
    v = rng.standard_normal(shape, dtype=np.float32) * np.exp2(rng.integers(-12, 13, shape)).astype(np.float32)
    if cols: v *= np.repeat(np.exp2(rng.integers(-cols, cols + 1, shape[:-2] + (1, shape[-1] // 4))) * (rng.random(shape[:-2] + (1, shape[-1] // 4)) > 0.0625), 4, axis=-1).astype(np.float32)
    return mx_ref.flush(v.astype(BF))
T, CAPP, OC, UN = 128, 16, 56, 32
HOST = [0 if c < 128 else 1 for c in CORES]
def term(a, B):
    return np.stack([mx_ref.matmul(mx_ref.quantize(a[:, 512 * i:512 * i + 512]), B) for i in range(4)], axis=2).reshape(128, -1)
def padded(e, k):
    return table(np.concatenate([e, np.full(k - len(e), -1)]))
def lists(rng, fixed=False, blocks=False, plain=False, short=False):
    own = [[[] for d in range(N)] for r in range(N)]
    union = np.full((N, 2, UN), -1)
    for d in range(N):
        half = np.arange(OC) if blocks else rng.permutation(OC)
        ext = [rng.choice(half[(1 - g) * (OC // 2):(2 - g) * (OC // 2)], UN - OC // 2, replace=False) for g in range(2)]
        low = int(rng.integers(0, 2)) if short else -1
        for g in range(2):
            R = [r for r in range(N) if HOST[r] == g]
            mine = list(half[g * (OC // 2):(g + 1) * (OC // 2)]) + list(ext[g])
            p = rng.permutation(len(R)); named = [set() for _ in mine]
            for k in range(CAPP):
                if not fixed: p = rng.permutation(len(R))
                for i in range(len(R) // 2): named[k * (len(R) // 2) + i] = {R[p[2 * i]], R[p[2 * i + 1]]}
            if g == low:
                both = [j for j in range(UN) if j >= OC // 2 or mine[j] in ext[1 - g]]
                for j in both:
                    for r in list(named[j]):
                        to = [t for t in range(OC // 2) if t not in both and r not in named[t]]
                        named[j].remove(r); named[rng.choice(to)].add(r)
            elif not (plain or fixed or short):
                for j in range(OC // 2, UN):
                    for r in list(rng.permutation(list(named[j])))[:rng.integers(0, 3)]:
                        to = [t for t in range(OC // 2) if r not in named[t]]
                        named[j].remove(r); named[rng.choice(to)].add(r)
            at = rng.permutation(UN)
            for j, s in enumerate(named):
                if s: union[d, g, at[j]] = mine[j]
                for r in s: own[r][d].append((mine[j], at[j]))
    send, place, un = [], np.full((N, N, CAPP), -1), []
    for r in range(N):
        send.append(table(rng.permutation(T))); u = []
        for d in range(N):
            o = [own[r][d][i] for i in rng.permutation(CAPP)]
            place[d, r] = [v for v, _ in o]; u += [w for _, w in o]
        un.append(table(u))
    return {"send": np.stack(send), "place": np.stack([table(place[d].reshape(-1)) for d in range(N)]), "un": np.stack(un), "upl": np.stack([padded(union[d].reshape(-1), 64) for d in range(N)])}
def setup_inputs(rng):
    return {"a": f(rng, N, 128, 4 * 512), "b": f(rng, N, 128, 4 * T), **lists(rng)}
def setup_inputs_blocks(rng):
    return {**setup_inputs(rng), **lists(rng, blocks=True, plain=True)}
def setup_inputs_lossless(rng):
    d = setup_inputs(rng)
    a = np.zeros((N, 128, 4 * 128, 4), np.float32)
    for r in range(N):
        k = rng.integers(0, 512, size=4 * 128)
        a[r, k // 4, np.arange(4 * 128), k % 4] = 1.0
    size = 2.0 ** rng.integers(-4, 5, size=(N, OC)); b = rng.integers(-1, 2, size=(N, 128, T, 4)).astype(np.float64)
    for r in range(N):
        s = entries(d["send"][r]).reshape(N, CAPP)
        for o in range(N): b[r][:, s[o]] *= size[o][entries(d["place"][o]).reshape(N, CAPP)[r]][None, :, None]
    d["a"], d["b"] = a.reshape(N, 128, 4 * 512).astype(BF), b.reshape(N, 128, 4 * T).astype(np.float32).astype(BF)
    return d
def setup_inputs_pairs(rng):
    return {**setup_inputs(rng), **lists(rng, fixed=True)}
def setup_inputs_short(rng):
    return {**setup_inputs(rng), **lists(rng, short=True)}
def setup_inputs_spread(rng):
    d = setup_inputs(rng); d["b"] = wide(rng, N, 128, 4 * T); return d
def check_inputs(x):
    b = []
    seen = np.zeros((N, OC), int)
    for r in range(N):
        s, u = entries(x["send"][r]), entries(x["un"][r]).reshape(N, CAPP)
        if sorted(s.tolist()) != list(range(T)): b.append("send")
        if u.min() < 0 or u.max() >= UN: b.append("un")
        for o in range(N):
            p = entries(x["place"][o]).reshape(N, CAPP)[r]
            if p.min() < 0 or p.max() >= OC or len(set(p.tolist())) != CAPP: b.append("place")
            w = entries(x["upl"][o])[:2 * UN].reshape(2, UN)[HOST[r]]
            if (w[u[o]] != p).any(): b.append("upl")
            seen[o][p] += 1
    for o in range(N):
        for g in range(2):
            w = entries(x["upl"][o]); bad = w.min() < -1 or w.max() >= OC or (w[2 * UN:] != -1).any(); w = w[:2 * UN].reshape(2, UN)[g]; w = w[w >= 0]
            if len(set(w.tolist())) != len(w): b.append("upl twice")
    if seen.min() < 2: b.append("a column with fewer than two terms")
    return b
def reference(a, b, send, place, un, upl):
    Z = [term(a[r], mx_ref.quantize(b[r])).reshape(128, T, 4) for r in range(N)]
    y = np.zeros((N, 128, 4 * OC), np.float32)
    for o in range(N):
        parts = []
        for r in range(N):
            t = np.zeros((128, OC, 4), np.float32); t[:, entries(place[o]).reshape(N, CAPP)[r]] = Z[r][:, entries(send[r]).reshape(N, CAPP)[o]]
            parts.append(t.reshape(128, 4 * OC))
        y[o] = mx_ref.total(parts)
    return {"y": y}

@@ -1,0 +1,299 @@
+from concourse.bass import DstId, RemoteDMATransfer
+from concourse.mybir import dt, AluOpType, ActivationFunctionType
+
+UN, OC = 32, 56
+H = OC + UN
+SEC = 2 * UN + 128
+RX = 3 * SEC
+
+SCRATCH = {
+    "at": ("sbuf", [128, 2048], "bfloat16"),
+    "bt": ("sbuf", [128, 512], "bfloat16"),
+    "aq": ("sbuf", [128, 512], "float8_e4m3fn_x4"),
+    "asc": ("sbuf", [128, 512], "uint8"),
+    "bw": ("sbuf", [128, 1024], "bfloat16"),
+    "bq": ("sbuf", [128, 256], "float8_e4m3fn_x4"),
+    "bsc": ("sbuf", [128, 256], "uint8"),
+    "dn": ("sbuf", [128, 512], "bfloat16"),
+    "dg": ("sbuf", [128, 516], "bfloat16"),
+    "one": ("sbuf", [128, 128], "bfloat16"),
+    "ex": ("sbuf", [128, RX + 160], "float8_e4m3fn_x4"),
+    "exs": ("sbuf", [128, RX + 160], "uint8"),
+    "zt": ("sbuf", [128, 1024], "bfloat16"),
+    "zq": ("sbuf", [128, 256], "float8_e4m3fn_x4"),
+    "zs": ("sbuf", [128, 256], "uint8"),
+    "ct": ("sbuf", [128, 512], "bfloat16"),
+    "cq": ("sbuf", [128, 128], "float8_e4m3fn_x4"),
+    "cs": ("sbuf", [128, 128], "uint8"),
+    "li": ("sbuf", [128, 16], "int32"),
+    "lx": ("sbuf", [128, 16], "int32"),
+    "base": ("sbuf", [128, 16], "int32"),
+    "oc": ("sbuf", [128, 32], "uint16"),
+    "ol": ("sbuf", [128, 32], "uint16"),
+    "up": ("sbuf", [128, 4], "int32"),
+    "pidx": ("sbuf", [128, 4], "int32"),
+    "pm": ("sbuf", [128, 4], "int32"),
+    "kc": ("sbuf", [128, 4], "int32"),
+    "rb": ("sbuf", [128, 4], "int32"),
+    "neg": ("sbuf", [128, 4], "int32"),
+    "po": ("sbuf", [128, 4], "uint16"),
+    "q4": ("sbuf", [128, 4], "int32"),
+    "q4f": ("sbuf", [128, 4], "float32"),
+    "p3": ("sbuf", [128, 4], "int32"),
+    "p3f": ("sbuf", [128, 4], "float32"),
+    "sv": ("sbuf", [128, 2 * UN], "float32"),
+    "uc": ("sbuf", [128, 2 * H], "float32"),
+    "ix": ("sbuf", [128, 2 * H], "float32"),
+    "i2": ("sbuf", [128, H], "float32"),
+    "i3": ("sbuf", [128, H // 2], "float32"),
+    "fo": ("sbuf", [128, H // 2], "uint16"),
+    "wl": ("sbuf", [128, 136], "float32"),
+    "wr": ("sbuf", [128, 136], "float32"),
+    "gl": ("sbuf", [128, 224], "float32"),
+    "yt": ("sbuf", [128, 224], "float32"),
+    "ps": ("psum", [128, 4096], "float32"),
+}
+SEMAPHORES = ["v", "s", "t", "gp", "ldl", "ldb", "lda0", "lda1", "ldu", "st", "ls",
+              "rc0", "rc1", "rc2", "rl0", "rl1", "rl2", "rr"]
+
+ADD, MUL, AND, SHR, LT, EQ = (AluOpType.add, AluOpType.mult, AluOpType.bitwise_and, AluOpType.arith_shift_right,
+                              AluOpType.is_lt, AluOpType.is_equal)
+COPY = ActivationFunctionType.Copy
+
+
+def rank_program(g, core, T, topo):
+    rank = T.rank_of(core)
+    if rank is None:
+        return
+    V, S, PE, SY = g.vector, g.scalar, g.tensor, g.sync
+    sem = T.sem
+    mine = [c for c in T.cores if topo.host(c) == topo.host(core)]
+    other = [c for c in T.cores if topo.host(c) != topo.host(core)]
+    kr = mine.index(core)
+    hm = T.rank_of(mine[0])
+    ho = T.rank_of(other[0])
+    gm = 0 if topo.host(core) == topo.host(T.cores[0]) else 1
+    go = 1 - gm
+
+    tick = {"v": 0, "s": 0, "t": 0, "gp": 0}
+    seen = {}
+
+    def did(name, ins):
+        ins.then_inc(sem[name], 1)
+        tick[name] += 1
+        return (name, tick[name])
+
+    def need(qn, *ticks):
+        q = {"v": V, "s": S, "t": PE, "g": g, "y": SY}[qn]
+        for name, n in ticks:
+            if seen.get((qn, name), 0) < n:
+                seen[(qn, name)] = n
+                q.wait_ge(sem[name], n)
+
+    def copy(qn, out, in_, *ticks):
+        need(qn, *ticks)
+        return did(qn, S.activation(out, in_, COPY) if qn == "s" else V.tensor_copy(out, in_))
+
+    def iota(out, pattern, base, cm=0, fl=False):
+        return did("gp", g.iota(out, pattern, base, cm, allow_small_or_imprecise_dtypes=True) if fl
+                   else g.iota(out, pattern, base, cm))
+
+    def load_up(q, r):
+        q.dma_start(T.up[r:r + 16, :], T.upl[:]).then_inc(sem.ldu, 16)
+
+    for r in (0, 16):
+        SY.dma_start(T.li[r:r + 16, 0:8], T.send[:]).then_inc(sem.ldl, 16)
+        S.dma_start(T.li[r:r + 16, 8:16], T.un[:]).then_inc(sem.ldl, 16)
+    S.dma_start(T.bt[:], T.b[:]).then_inc(sem.ldb, 16)
+    load_up(SY, 0)
+    SY.dma_start(T.at[:, 0:1536], T.a[:, 0:1536]).then_inc(sem.lda0, 16)
+    load_up(S, 16)
+    S.dma_start(T.at[:, 1536:2048], T.a[:, 1536:2048]).then_inc(sem.lda1, 16)
+    need("y", ("lda1", 16))
+    for r in range(32, 128, 16):
+        load_up(SY, r)
+    LDL, LDB, LDU = ("ldl", 64), ("ldb", 16), ("ldu", 128)
+
+    z_bw = did("v", V.memset(T.bw[:, 0:512], 0.0))
+    did("v", V.memset(T.one[:], 1.0))
+    z_dg = did("v", V.memset(T.dg[:], 0.0))
+    did("v", V.memset(T.zt[:, 384:512], 0.0))
+    did("v", V.memset(T.zt[:, 896:1024], 0.0))
+    b_base = iota(T.base[:, 8:16], [[UN, 4], [UN, 2]] if hm < ho else [[UN, 4], [-UN, 2]], -UN * kr - (UN if hm < ho else 0))
+    b_zero = iota(T.base[:, 0:8], [[0, 8]], 0)
+    iota(T.pidx[:], [[0, 4]], 0, 1)
+    iota(T.kc[:], [[0, 2], [16, 2]], OC + 1)
+    iota(T.rb[:], [[H, 2], [0, 2]], 0)
+    need("g", z_dg)
+    diag = did("gp", g.affine_select(T.dg[:, 3:515:4], T.one[:], [[-1, 128]], EQ, 0.0, 0, 1))
+    iota(T.sv[:], [[0, 2], [1, UN]], 0, 0, True)
+    iota(T.uc[:], [[0, H // 2], [1, 4]], 0, 0, True)
+    iota(T.ix[:], [[0, 2 * H]], UN, 0, True)
+    iota(T.wl[:, 128:136], [[0, 8]], 0, 0, True)
+    c_all = iota(T.wr[:, 128:136], [[0, 8]], 0, 0, True)
+    copy("s", T.bw[:, 512:1024], T.bw[:, 0:512], z_bw)
+
+    need("v", b_base)
+    did("v", V.tensor_scalar(T.base[:, 8:16], T.base[:, 8:16], 127, None, op0=AND))
+
+    def E(b):
+        o = SEC * b + UN
+        return T.ex[:, o:o + 128], T.exs[:, o:o + 128]
+
+    e_all = [None]
+
+    def make_e(b):
+        need("v", diag)
+        c, s = E(b)
+        e_all[0] = did("v", V.quantize_mx(c, s, T.dg[:, 3 - b:3 - b + 512]))
+
+    need("v", LDL, b_zero)
+    x = copy("v", T.li[32:64, :], T.li[0:32, :])
+    need("v", x)
+    for r in (0, 64):
+        x = did("v", V.tensor_tensor(T.lx[r:r + 64, :], T.li[0:64, :], T.base[0:64, :], ADD))
+    need("v", x)
+
+    def offsets(out, h, at, t, k):
+        return did("v", V.tensor_scalar(out[:, at:at + 7 * k + 1:k], T.lx[:, h:16:2], 4, t, op0=MUL, op1=ADD))
+
+    oc = [offsets(T.oc, ho, 16 * (t // 2) + t % 2, t, 2) for t in range(4)]
+    dn_c = [copy("s", T.dn[:, 128 * u:128 * u + 128], T.bt[:, 0:512].indirect(T.oc[:, 16 * u:16 * u + 8]), LDB, oc[2 * u + 1])
+            for u in (0, 1)]
+    ol = [offsets(T.ol, hm, t, t, 4) for t in range(4)]
+    dn_l = copy("s", T.dn[:, 256:512], T.bt[:, 0:512].indirect(T.ol[:, 0:16]), ol[3])
+    for u in (0, 1):
+        x = copy("v", T.bw[:, 0:512].indirect(T.oc[:, 16 * u + 8:16 * u + 16]), T.dn[:, 128 * u:128 * u + 128],
+                 oc[2 * u + 1], x, dn_c[u])
+    need("v", x)
+    b_c = did("v", V.quantize_mx(T.bq[:, 0:128], T.bsc[:, 0:128], T.bw[:, 0:512]))
+
+    a_q = []
+    for i in range(4):
+        need("v", ("lda%d" % (i // 3), 16))
+        a_q.append(did("v", V.quantize_mx(T.aq[:, 128 * i:128 * i + 128], T.asc[:, 128 * i:128 * i + 128],
+                                          T.at[:, 512 * i:512 * i + 512])))
+
+    def own(i, half, bank, stop):
+        need("t", a_q[i], b_c)
+        return did("t", PE.matmul_mx(T.ps[:, 512 * bank:512 * bank + 128],
+                                     T.aq[:, 128 * i:128 * i + 128], T.asc[:, 128 * i:128 * i + 128],
+                                     T.bq[:, 128 * half:128 * half + 128], T.bsc[:, 128 * half:128 * half + 128],
+                                     True, stop))
+
+    def unpack(b, col, bank, start, stop):
+        c, s = E(b)
+        need("t", e_all[0])
+        return did("t", PE.matmul_mx(T.ps[:, 512 * bank:512 * bank + 128], c, s,
+                                     T.ex[:, col:col + 128], T.exs[:, col:col + 128], start, stop))
+
+    def ps(bank, lo, hi):
+        return T.ps[:, 512 * bank + lo:512 * bank + hi]
+
+    zc = [own(i, 0, i, True) for i in range(4)]
+    for i in range(4):
+        own(i, 0, 4 + i, False)
+    cp = [copy("s", T.zt[:, i:384:4], ps(i, UN, 128), zc[i]) for i in range(4)]
+    make_e(0)
+    make_e(1)
+    need("v", *cp)
+    zq_c = did("v", V.quantize_mx(T.zq[:, 0:128], T.zs[:, 0:128], T.zt[:, 0:512]))
+
+    peers = [mine[(kr + 1 + j) % 4] for j in range(3)]
+    sent = [0]
+
+    def put(dst_core, dst, src, name):
+        rid, pid = topo.addr(dst_core, core)
+        g.remote_dma(dst, src, sem[name], sem.ls, pid, rid, topo.mask(core, dst_core))
+        sent[0] += len(topo.engines(core, dst_core))
+
+    def hop1(name, col, at):
+        for j in range(3):
+            o, c = SEC * (2 - j) + at, col + UN * j
+            put(peers[j], T.ex[:, o:o + UN].bitcast(dt.uint8), T.zq[:, c:c + UN].bitcast(dt.uint8), name + str(2 - j))
+            put(peers[j], T.exs[:, o:o + UN], T.zs[:, c:c + UN], name + str(2 - j))
+
+    def got(name, s):
+        return (name + str(s), 2 * len(topo.engines(mine[(kr + 1 + s) % 4], core)))
+
+    need("g", zq_c)
+    hop1("rc", 0, 0)
+
+    need("v", copy("v", T.bw[:, 512:1024].indirect(T.ol[:, 16:32]), T.dn[:, 256:512], ol[3], dn_l))
+    b_l = did("v", V.quantize_mx(T.bq[:, 128:256], T.bsc[:, 128:256], T.bw[:, 512:1024]))
+    did("v", V.memset(T.ct[:, 128:512], 0.0))
+    make_e(2)
+    make_e(3)
+    need("t", b_l)
+    zl = []
+    for i in range(4):
+        need("t", cp[i])
+        zl.append(own(i, 1, i, True))
+    lp = [copy("svsv"[i], T.zt[:, 512 + i:896:4], ps(i, 0, 96), zl[i]) for i in range(4)]
+    need("v", *lp)
+    zq_l = did("v", V.quantize_mx(T.zq[:, 128:256], T.zs[:, 128:256], T.zt[:, 512:1024]))
+    need("g", zq_l)
+    hop1("rl", 128, UN + 128)
+
+    need("v", LDU, c_all)
+    did("v", V.tensor_scalar(T.neg[:], T.up[:], 0, None, op0=LT))
+    did("v", V.tensor_scalar(T.pm[:], T.pidx[:], 15, None, op0=AND))
+    did("v", V.tensor_scalar(T.q4[:], T.pidx[:], 15, 2, op0=AND, op1=SHR))
+    did("v", V.tensor_scalar(T.p3[:], T.pidx[:], 3, None, op0=AND))
+    need("v", did("v", V.tensor_tensor(T.rb[:], T.rb[:], T.up[:], ADD)))
+    x = did("v", V.tensor_tensor(T.kc[:], T.kc[:], T.pm[:], ADD))
+    copy("v", T.q4f[:], T.q4[:])
+    need("v", x)
+    x = did("v", V.tensor_tensor(T.neg[:], T.neg[:], T.kc[:], MUL))
+    copy("v", T.p3f[:], T.p3[:])
+    need("v", x)
+    x = did("v", V.tensor_tensor(T.rb[:], T.rb[:], T.neg[:], ADD))
+    did("v", V.tensor_scalar(T.uc[:], T.uc[:], T.q4f[:, 0:1], None, op0=EQ))
+    need("v", x)
+    po = copy("v", T.po[:], T.rb[:])
+
+    last = [None] * 4
+    for s in (2, 1, 0):
+        need("t", got("rc", s))
+        for b in range(4):
+            last[b] = unpack(b, SEC * s, 4 + b, False, s == 0)
+    cc = [copy("svsv"[b], T.ct[:, b:128:4], ps(4 + b, 0, UN), last[b]) for b in range(4)]
+    need("v", *cc)
+    c_q = did("v", V.quantize_mx(T.cq[:], T.cs[:], T.ct[:]))
+
+    far = other[kr]
+    need("g", c_q)
+    put(far, T.ex[:, RX:RX + UN].bitcast(dt.uint8), T.cq[:, 0:UN].bitcast(dt.uint8), "rr")
+    put(far, T.exs[:, RX:RX + UN], T.cs[:, 0:UN], "rr")
+
+    need("v", po)
+    need("v", copy("v", T.ix[:, 0:2 * H].indirect(T.po[:, 0:4]), T.sv[:]))
+    need("v", did("v", V.tensor_tensor(T.ix[:], T.ix[:], T.uc[:], MUL)))
+    need("v", did("v", V.tensor_tensor(T.i2[:], T.ix[:, 0:2 * H:2], T.ix[:, 1:2 * H:2], ADD)))
+    need("v", did("v", V.tensor_tensor(T.i3[:], T.i2[:, 0:H:2], T.i2[:, 1:H:2], ADD)))
+    fo = did("v", V.tensor_scalar(T.fo[:], T.i3[:], 4.0, T.p3f[:, 0:1], op0=MUL, op1=ADD))
+
+    for i in range(4):
+        need("t", lp[i])
+        own(i, 1, i, False)
+    for s in (2, 1, 0):
+        need("t", got("rl", s))
+        for b in range(4):
+            last[b] = unpack(b, SEC * s + 2 * UN, b, False, s == 0)
+    wl = [copy("s", T.wl[:, b:128:4], ps(b, 96, 128), last[b]) for b in range(4)]
+    q = H // 4
+    gl = copy("s", T.gl[:], T.wl[:, 0:136].indirect(T.fo[:, q * gm:q * gm + OC // 4]), fo, c_all, *wl)
+
+    need("t", ("rr", 2 * len(topo.engines(far, core))))
+    rc = []
+    for b in range(4):
+        need("t", cc[b])
+        rc.append(unpack(b, RX, 4 + b, True, True))
+    wr = [copy("v", T.wr[:, b:128:4], ps(4 + b, 0, UN), rc[b]) for b in range(4)]
+    need("v", fo, gl, *wr)
+    y = did("v", V.tensor_tensor(T.yt[:], T.wr[:, 0:136].indirect(T.fo[:, q * go:q * go + OC // 4]), T.gl[:], ADD))
+    need("y", y)
+    SY.dma_start(T.y[:], T.yt[:]).then_inc(sem.st, 16)
+    SY.wait_ge(sem.st, 16)
+    g.wait_ge(sem.ls, sent[0])
+    need("g", ("v", tick["v"]), ("s", tick["s"]), ("t", tick["t"]))

@@ -2,9 +2,10 @@ from concourse.bass import DstId, RemoteDMATransfer
 from concourse.mybir import dt, AluOpType, ActivationFunctionType
 
 UN, OC = 32, 56
-H = OC + UN
-SEC = 2 * UN + 128
-RX = 3 * SEC
+XL, XE, XS, XR = 0, 3 * UN, 3 * UN + 512, 6 * UN + 512
+TR = 4 * (UN + 1)
+KEEP = 128
+NX = OC + UN
 
 SCRATCH = {
     "at": ("sbuf", [128, 2048], "bfloat16"),
@@ -17,12 +18,11 @@ SCRATCH = {
     "dn": ("sbuf", [128, 512], "bfloat16"),
     "dg": ("sbuf", [128, 516], "bfloat16"),
     "one": ("sbuf", [128, 128], "bfloat16"),
-    "ex": ("sbuf", [128, RX + 160], "float8_e4m3fn_x4"),
-    "exs": ("sbuf", [128, RX + 160], "uint8"),
+    "ex": ("sbuf", [128, XR + UN], "float8_e4m3fn_x4"),
+    "exs": ("sbuf", [128, XR + UN], "uint8"),
     "zt": ("sbuf", [128, 1024], "bfloat16"),
     "zq": ("sbuf", [128, 256], "float8_e4m3fn_x4"),
     "zs": ("sbuf", [128, 256], "uint8"),
-    "ct": ("sbuf", [128, 512], "bfloat16"),
     "cq": ("sbuf", [128, 128], "float8_e4m3fn_x4"),
     "cs": ("sbuf", [128, 128], "uint8"),
     "li": ("sbuf", [128, 16], "int32"),
@@ -31,52 +31,42 @@ SCRATCH = {
     "oc": ("sbuf", [128, 32], "uint16"),
     "ol": ("sbuf", [128, 32], "uint16"),
     "up": ("sbuf", [128, 4], "int32"),
+    "um": ("sbuf", [128, 4], "int32"),
+    "kc": ("sbuf", [128, 4], "int32"),
+    "po": ("sbuf", [128, 4], "uint16"),
+    "pg": ("sbuf", [128, 4], "uint16"),
     "pidx": ("sbuf", [128, 4], "int32"),
     "pm": ("sbuf", [128, 4], "int32"),
-    "kc": ("sbuf", [128, 4], "int32"),
-    "rb": ("sbuf", [128, 4], "int32"),
-    "neg": ("sbuf", [128, 4], "int32"),
-    "po": ("sbuf", [128, 4], "uint16"),
-    "q4": ("sbuf", [128, 4], "int32"),
-    "q4f": ("sbuf", [128, 4], "float32"),
-    "p3": ("sbuf", [128, 4], "int32"),
-    "p3f": ("sbuf", [128, 4], "float32"),
+    "pa": ("sbuf", [128, 4], "float32"),
+    "pc": ("sbuf", [128, 4], "float32"),
     "sv": ("sbuf", [128, 2 * UN], "float32"),
-    "uc": ("sbuf", [128, 2 * H], "float32"),
-    "ix": ("sbuf", [128, 2 * H], "float32"),
-    "i2": ("sbuf", [128, H], "float32"),
-    "i3": ("sbuf", [128, H // 2], "float32"),
-    "fo": ("sbuf", [128, H // 2], "uint16"),
-    "wl": ("sbuf", [128, 136], "float32"),
-    "wr": ("sbuf", [128, 136], "float32"),
-    "gl": ("sbuf", [128, 224], "float32"),
-    "yt": ("sbuf", [128, 224], "float32"),
+    "ka": ("sbuf", [128, NX], "float32"),
+    "ix": ("sbuf", [128, NX + 512], "float32"),
+    "sc": ("sbuf", [128, NX], "float32"),
+    "fo": ("sbuf", [128, NX // 4], "uint16"),
+    "tw": ("sbuf", [128, TR + 4 * UN], "float32"),
+    "al": ("sbuf", [128, 4 * UN], "float32"),
+    "yt": ("sbuf", [128, 4 * OC], "float32"),
     "ps": ("psum", [128, 4096], "float32"),
 }
-SEMAPHORES = ["v", "s", "t", "gp", "ldl", "ldb", "lda0", "lda1", "ldu", "st", "ls",
-              "rc0", "rc1", "rc2", "rl0", "rl1", "rl2", "rr"]
+SEMAPHORES = ["v", "s", "t", "gp", "ldl", "ldb", "lda0", "lda1", "lda2", "ldu", "st", "ls",
+              "rc0", "rc1", "rc2", "rl0", "rl1", "rl2", "rr", "re"]
 
-ADD, MUL, AND, SHR, LT, EQ = (AluOpType.add, AluOpType.mult, AluOpType.bitwise_and, AluOpType.arith_shift_right,
-                              AluOpType.is_lt, AluOpType.is_equal)
+ADD, SUB, MUL, AND, MIN, MAX, EQ = (AluOpType.add, AluOpType.subtract, AluOpType.mult, AluOpType.bitwise_and,
+                                    AluOpType.min, AluOpType.max, AluOpType.is_equal)
 COPY = ActivationFunctionType.Copy
 
 
+def helper_of(core, topo):
+    return [c for c in topo.cores_of(core) if c != core and topo.die(c) == topo.die(core)][0]
+
+
 def rank_program(g, core, T, topo):
-    rank = T.rank_of(core)
-    if rank is None:
-        return
     V, S, PE, SY = g.vector, g.scalar, g.tensor, g.sync
     sem = T.sem
-    mine = [c for c in T.cores if topo.host(c) == topo.host(core)]
-    other = [c for c in T.cores if topo.host(c) != topo.host(core)]
-    kr = mine.index(core)
-    hm = T.rank_of(mine[0])
-    ho = T.rank_of(other[0])
-    gm = 0 if topo.host(core) == topo.host(T.cores[0]) else 1
-    go = 1 - gm
-
     tick = {"v": 0, "s": 0, "t": 0, "gp": 0}
     seen = {}
+    sent = [0]
 
     def did(name, ins):
         ins.then_inc(sem[name], 1)
@@ -98,84 +88,107 @@ def rank_program(g, core, T, topo):
         return did("gp", g.iota(out, pattern, base, cm, allow_small_or_imprecise_dtypes=True) if fl
                    else g.iota(out, pattern, base, cm))
 
-    def load_up(q, r):
-        q.dma_start(T.up[r:r + 16, :], T.upl[:]).then_inc(sem.ldu, 16)
+    def put(dst_core, dst, src, name):
+        rid, pid = topo.addr(dst_core, core)
+        g.remote_dma(dst, src, sem[name], sem.ls, pid, rid, topo.mask(core, dst_core))
+        sent[0] += len(topo.engines(core, dst_core))
+
+    def E(b):
+        o = XE + 128 * b
+        return T.ex[:, o:o + 128], T.exs[:, o:o + 128]
+
+    rank = T.rank_of(core)
+    if rank is None:
+        served = [c for c in T.cores if helper_of(c, topo) == core]
+        if served:
+            did("v", V.memset(T.one[:], 1.0))
+            need("g", did("v", V.memset(T.dg[:], 0.0)))
+            need("v", did("gp", g.affine_select(T.dg[:, 3:515:4], T.one[:], [[-1, 128]], EQ, 0.0, 0, 1)))
+            need("g", *[did("v", V.quantize_mx(*E(b), T.dg[:, 3 - b:3 - b + 512])) for b in range(4)])
+            put(served[0], T.ex[:, XE:XS].bitcast(dt.uint8), T.ex[:, XE:XS].bitcast(dt.uint8), "re")
+            put(served[0], T.exs[:, XE:XS], T.exs[:, XE:XS], "re")
+            g.wait_ge(sem.ls, sent[0])
+        return
+
+    mine = [c for c in T.cores if topo.host(c) == topo.host(core)]
+    other = [c for c in T.cores if topo.host(c) != topo.host(core)]
+    kr = mine.index(core)
+    hm = T.rank_of(mine[0])
+    ho = T.rank_of(other[0])
+    gm = 0 if topo.host(core) == topo.host(T.cores[0]) else 1
+    go = 1 - gm
+    ka, kb = kr ^ 1, 2 - 2 * (kr // 2)
+    pos = {ka: 0, kb: 1, kb + 1: 2, kr: 3}
 
     for r in (0, 16):
         SY.dma_start(T.li[r:r + 16, 0:8], T.send[:]).then_inc(sem.ldl, 16)
         S.dma_start(T.li[r:r + 16, 8:16], T.un[:]).then_inc(sem.ldl, 16)
     S.dma_start(T.bt[:], T.b[:]).then_inc(sem.ldb, 16)
-    load_up(SY, 0)
-    SY.dma_start(T.at[:, 0:1536], T.a[:, 0:1536]).then_inc(sem.lda0, 16)
-    load_up(S, 16)
-    S.dma_start(T.at[:, 1536:2048], T.a[:, 1536:2048]).then_inc(sem.lda1, 16)
-    need("y", ("lda1", 16))
-    for r in range(32, 128, 16):
-        load_up(SY, r)
+    for k, (lo, hi) in enumerate(((0, 512), (512, 1536), (1536, 2048))):
+        SY.dma_start(T.at[:, lo:hi], T.a[:, lo:hi]).then_inc(sem["lda%d" % k], 16)
+    for r in range(0, 128, 16):
+        SY.dma_start(T.up[r:r + 16, :], T.upl[:]).then_inc(sem.ldu, 16)
     LDL, LDB, LDU = ("ldl", 64), ("ldb", 16), ("ldu", 128)
 
+    z_base = did("v", V.memset(T.base[:], 0))
     z_bw = did("v", V.memset(T.bw[:, 0:512], 0.0))
-    did("v", V.memset(T.one[:], 1.0))
-    z_dg = did("v", V.memset(T.dg[:], 0.0))
-    did("v", V.memset(T.zt[:, 384:512], 0.0))
-    did("v", V.memset(T.zt[:, 896:1024], 0.0))
-    b_base = iota(T.base[:, 8:16], [[UN, 4], [UN, 2]] if hm < ho else [[UN, 4], [-UN, 2]], -UN * kr - (UN if hm < ho else 0))
-    b_zero = iota(T.base[:, 0:8], [[0, 8]], 0)
-    iota(T.pidx[:], [[0, 4]], 0, 1)
-    iota(T.kc[:], [[0, 2], [16, 2]], OC + 1)
-    iota(T.rb[:], [[H, 2], [0, 2]], 0)
-    need("g", z_dg)
-    diag = did("gp", g.affine_select(T.dg[:, 3:515:4], T.one[:], [[-1, 128]], EQ, 0.0, 0, 1))
-    iota(T.sv[:], [[0, 2], [1, UN]], 0, 0, True)
-    iota(T.uc[:], [[0, H // 2], [1, 4]], 0, 0, True)
-    iota(T.ix[:], [[0, 2 * H]], UN, 0, True)
-    iota(T.wl[:, 128:136], [[0, 8]], 0, 0, True)
-    c_all = iota(T.wr[:, 128:136], [[0, 8]], 0, 0, True)
+    did("v", V.memset(T.zt[:, 512:640], 0.0))
+    p_idx = iota(T.pidx[:], [[0, 4]], 0, 1 + KEEP)
+    need("g", z_base)
+    c = 8 + ho + 2 * (kb + 1)
+    b_base = iota(T.base[:, c:c + 1], [[0, 1]], UN)
+    if kr < 3:
+        b_base = iota(T.base[:, 8 + hm + 2 * (kr + 1):16:2], [[UN, 3 - kr]], UN)
+    if kr > 0:
+        b_base = iota(T.base[:, 8 + hm:8 + hm + 2 * kr:2], [[UN, kr]], UN * (4 - kr))
+    iota(T.kc[:], [[1, 4]], NX, 4)
+    iota(T.ka[:], [[0, NX // 4], [8 * KEEP, 4]], 0, 0, True)
+    iota(T.sv[:], [[UN + 1, 2], [1, UN]], 0, 0, True)
+    iota(T.ix[:, 0:OC], [[0, OC]], UN, 0, True)
+    c_all = iota(T.tw[:, 4 * UN:TR], [[0, 4]], 0, 0, True)
     copy("s", T.bw[:, 512:1024], T.bw[:, 0:512], z_bw)
+    need("v", p_idx)
+    need("v", did("v", V.tensor_scalar(T.pm[:], T.pidx[:], 3 + 12 * KEEP, None, op0=AND)))
+    did("v", V.tensor_scalar(T.pa[:], T.pm[:], 2, 4 * KEEP, op0=MUL, op1=ADD))
+    did("v", V.tensor_scalar(T.pc[:], T.pm[:], -12 * KEEP, None, op0=ADD))
 
-    need("v", b_base)
-    did("v", V.tensor_scalar(T.base[:, 8:16], T.base[:, 8:16], 127, None, op0=AND))
-
-    def E(b):
-        o = SEC * b + UN
-        return T.ex[:, o:o + 128], T.exs[:, o:o + 128]
-
-    e_all = [None]
-
-    def make_e(b):
-        need("v", diag)
-        c, s = E(b)
-        e_all[0] = did("v", V.quantize_mx(c, s, T.dg[:, 3 - b:3 - b + 512]))
-
-    need("v", LDL, b_zero)
-    x = copy("v", T.li[32:64, :], T.li[0:32, :])
-    need("v", x)
-    for r in (0, 64):
-        x = did("v", V.tensor_tensor(T.lx[r:r + 64, :], T.li[0:64, :], T.base[0:64, :], ADD))
+    need("v", LDL, b_base)
+    for r in range(0, 128, 32):
+        x = did("v", V.tensor_tensor(T.lx[r:r + 32, :], T.li[0:32, :], T.base[0:32, :], ADD))
     need("v", x)
 
-    def offsets(out, h, at, t, k):
-        return did("v", V.tensor_scalar(out[:, at:at + 7 * k + 1:k], T.lx[:, h:16:2], 4, t, op0=MUL, op1=ADD))
+    def offsets(out, h):
+        return [did("v", V.tensor_scalar(out[:, t:32:4], T.lx[:, h:16:2], 4, t, op0=MUL, op1=ADD)) for t in range(4)][3]
 
-    oc = [offsets(T.oc, ho, 16 * (t // 2) + t % 2, t, 2) for t in range(4)]
-    dn_c = [copy("s", T.dn[:, 128 * u:128 * u + 128], T.bt[:, 0:512].indirect(T.oc[:, 16 * u:16 * u + 8]), LDB, oc[2 * u + 1])
-            for u in (0, 1)]
-    ol = [offsets(T.ol, hm, t, t, 4) for t in range(4)]
-    dn_l = copy("s", T.dn[:, 256:512], T.bt[:, 0:512].indirect(T.ol[:, 0:16]), ol[3])
-    for u in (0, 1):
-        x = copy("v", T.bw[:, 0:512].indirect(T.oc[:, 16 * u + 8:16 * u + 16]), T.dn[:, 128 * u:128 * u + 128],
-                 oc[2 * u + 1], x, dn_c[u])
-    need("v", x)
-    b_c = did("v", V.quantize_mx(T.bq[:, 0:128], T.bsc[:, 0:128], T.bw[:, 0:512]))
+    oc = offsets(T.oc, ho)
+    pieces = [(ka, 1), (kb, 2), (kr, 1)]
+    dn_c = [copy("s", T.dn[:, 64 * pos[k]:64 * (pos[k] + n)], T.bt[:, 0:512].indirect(T.oc[:, 4 * k:4 * (k + n)]), LDB, oc)
+            for k, n in pieces]
+    ol = offsets(T.ol, hm)
+    dn_l = copy("s", T.dn[:, 256:512], T.bt[:, 0:512].indirect(T.ol[:, 0:16]), ol)
 
-    a_q = []
-    for i in range(4):
-        need("v", ("lda%d" % (i // 3), 16))
-        a_q.append(did("v", V.quantize_mx(T.aq[:, 128 * i:128 * i + 128], T.asc[:, 128 * i:128 * i + 128],
-                                          T.at[:, 512 * i:512 * i + 512])))
+    def scatter(u):
+        k, n = pieces[u]
+        return copy("v", T.bw[:, 128 * pos[k]:128 * (pos[k] + n)].indirect(T.oc[:, 16 + 4 * k:16 + 4 * (k + n)]),
+                    T.dn[:, 64 * pos[k]:64 * (pos[k] + n)], oc, dn_c[u])
 
-    def own(i, half, bank, stop):
-        need("t", a_q[i], b_c)
+    def quant_b(half, *ticks):
+        need("v", *ticks)
+        lo = 128 * half
+        return did("v", V.quantize_mx(T.bq[:, lo:lo + 128], T.bsc[:, lo:lo + 128], T.bw[:, 4 * lo:4 * lo + 512]))
+
+    def quant_a(i):
+        need("v", ("lda%d" % ((i + 1) // 2), 16))
+        return did("v", V.quantize_mx(T.aq[:, 128 * i:128 * i + 128], T.asc[:, 128 * i:128 * i + 128],
+                                      T.at[:, 512 * i:512 * i + 512]))
+
+    x = [scatter(0), scatter(1)]
+    a_q = [quant_a(0)]
+    b_c = quant_b(0, *x)
+    a_q += [quant_a(i) for i in (1, 2, 3)]
+
+    def own(i, half, bank, stop, *ticks):
+        need("t", a_q[i], *ticks)
         return did("t", PE.matmul_mx(T.ps[:, 512 * bank:512 * bank + 128],
                                      T.aq[:, 128 * i:128 * i + 128], T.asc[:, 128 * i:128 * i + 128],
                                      T.bq[:, 128 * half:128 * half + 128], T.bsc[:, 128 * half:128 * half + 128],
@@ -183,116 +196,103 @@ def rank_program(g, core, T, topo):
 
     def unpack(b, col, bank, start, stop):
         c, s = E(b)
-        need("t", e_all[0])
+        need("t", ("re", 2 * len(topo.engines(helper_of(core, topo), core))))
         return did("t", PE.matmul_mx(T.ps[:, 512 * bank:512 * bank + 128], c, s,
                                      T.ex[:, col:col + 128], T.exs[:, col:col + 128], start, stop))
 
     def ps(bank, lo, hi):
         return T.ps[:, 512 * bank + lo:512 * bank + hi]
 
-    zc = [own(i, 0, i, True) for i in range(4)]
-    for i in range(4):
-        own(i, 0, 4 + i, False)
-    cp = [copy("s", T.zt[:, i:384:4], ps(i, UN, 128), zc[i]) for i in range(4)]
-    make_e(0)
-    make_e(1)
+    zc = [own(i, 0, i, True, b_c) for i in range(4)]
+    cp = [copy("s", T.zt[:, 128 + i:512:4], ps(i, 0, 96), zc[i]) for i in range(4)]
+    need("v", b_c)
+    s_own = scatter(2)
     need("v", *cp)
-    zq_c = did("v", V.quantize_mx(T.zq[:, 0:128], T.zs[:, 0:128], T.zt[:, 0:512]))
+    zq_c = did("v", V.quantize_mx(T.zq[:, 0:128], T.zs[:, 0:128], T.zt[:, 128:640]))
 
     peers = [mine[(kr + 1 + j) % 4] for j in range(3)]
-    sent = [0]
-
-    def put(dst_core, dst, src, name):
-        rid, pid = topo.addr(dst_core, core)
-        g.remote_dma(dst, src, sem[name], sem.ls, pid, rid, topo.mask(core, dst_core))
-        sent[0] += len(topo.engines(core, dst_core))
 
     def hop1(name, col, at):
         for j in range(3):
-            o, c = SEC * (2 - j) + at, col + UN * j
+            o, c = at(2 - j), col(j)
             put(peers[j], T.ex[:, o:o + UN].bitcast(dt.uint8), T.zq[:, c:c + UN].bitcast(dt.uint8), name + str(2 - j))
             put(peers[j], T.exs[:, o:o + UN], T.zs[:, c:c + UN], name + str(2 - j))
 
     def got(name, s):
         return (name + str(s), 2 * len(topo.engines(mine[(kr + 1 + s) % 4], core)))
 
-    need("g", zq_c)
-    hop1("rc", 0, 0)
+    def xs(s):
+        return XS + UN * (2 - s)
 
-    need("v", copy("v", T.bw[:, 512:1024].indirect(T.ol[:, 16:32]), T.dn[:, 256:512], ol[3], dn_l))
-    b_l = did("v", V.quantize_mx(T.bq[:, 128:256], T.bsc[:, 128:256], T.bw[:, 512:1024]))
-    did("v", V.memset(T.ct[:, 128:512], 0.0))
-    make_e(2)
-    make_e(3)
-    need("t", b_l)
-    zl = []
+    def xl(s):
+        return XL + UN * s
+
+    need("g", zq_c)
+    hop1("rc", lambda j: UN * pos[(kr + 1 + j) % 4], xs)
+
+    b_own = quant_b(0, s_own)
     for i in range(4):
-        need("t", cp[i])
-        zl.append(own(i, 1, i, True))
-    lp = [copy("svsv"[i], T.zt[:, 512 + i:896:4], ps(i, 0, 96), zl[i]) for i in range(4)]
+        own(i, 0, 4 + i, False, b_own)
+
+    b_l = quant_b(1, copy("v", T.bw[:, 512:1024].indirect(T.ol[:, 16:32]), T.dn[:, 256:512], ol, dn_l))
+    zl = [own(i, 1, i, True, b_l, cp[i]) for i in range(4)]
+    lp = [copy("s", T.zt[:, 640 + i:1024:4], ps(i, UN, 128), zl[i]) for i in range(4)]
+    for i in range(4):
+        own(i, 1, i, False, lp[i])
+
+    need("v", LDU, c_all)
+    x = did("v", V.tensor_scalar(T.um[:], T.up[:], 1023, None, op0=AND))
+    did("v", V.tensor_scalar(T.ka[:], T.ka[:], T.pa[:, 0:1], KEEP, op0=SUB, op1=MIN))
+    need("v", x)
+    x = did("v", V.tensor_tensor(T.um[:], T.um[:], T.kc[:], MIN))
+    copy("v", T.pg[:], T.up[:])
+    x = copy("v", T.po[:], T.um[:], x)
+
+    def place(h, lo, *ticks):
+        return copy("v", T.ix[:, 0:NX + 512].indirect(T.po[:, 2 * h:2 * h + 2]), T.sv[:, lo:lo + UN], *ticks)
+
+    ix = place(gm, 0, x)
+
     need("v", *lp)
     zq_l = did("v", V.quantize_mx(T.zq[:, 128:256], T.zs[:, 128:256], T.zt[:, 512:1024]))
     need("g", zq_l)
-    hop1("rl", 128, UN + 128)
-
-    need("v", LDU, c_all)
-    did("v", V.tensor_scalar(T.neg[:], T.up[:], 0, None, op0=LT))
-    did("v", V.tensor_scalar(T.pm[:], T.pidx[:], 15, None, op0=AND))
-    did("v", V.tensor_scalar(T.q4[:], T.pidx[:], 15, 2, op0=AND, op1=SHR))
-    did("v", V.tensor_scalar(T.p3[:], T.pidx[:], 3, None, op0=AND))
-    need("v", did("v", V.tensor_tensor(T.rb[:], T.rb[:], T.up[:], ADD)))
-    x = did("v", V.tensor_tensor(T.kc[:], T.kc[:], T.pm[:], ADD))
-    copy("v", T.q4f[:], T.q4[:])
-    need("v", x)
-    x = did("v", V.tensor_tensor(T.neg[:], T.neg[:], T.kc[:], MUL))
-    copy("v", T.p3f[:], T.p3[:])
-    need("v", x)
-    x = did("v", V.tensor_tensor(T.rb[:], T.rb[:], T.neg[:], ADD))
-    did("v", V.tensor_scalar(T.uc[:], T.uc[:], T.q4f[:, 0:1], None, op0=EQ))
-    need("v", x)
-    po = copy("v", T.po[:], T.rb[:])
+    hop1("rl", lambda j: 128 + UN * (j + 1), xl)
 
     last = [None] * 4
     for s in (2, 1, 0):
         need("t", got("rc", s))
         for b in range(4):
-            last[b] = unpack(b, SEC * s, 4 + b, False, s == 0)
-    cc = [copy("svsv"[b], T.ct[:, b:128:4], ps(4 + b, 0, UN), last[b]) for b in range(4)]
+            last[b] = unpack(b, xs(s) - 96, 4 + b, False, s == 0)
+    cc = [copy("svsv"[b], T.zt[:, b:128:4], ps(4 + b, 96, 128), last[b]) for b in range(4)]
     need("v", *cc)
-    c_q = did("v", V.quantize_mx(T.cq[:], T.cs[:], T.ct[:]))
+    c_q = did("v", V.quantize_mx(T.cq[:], T.cs[:], T.zt[:, 0:512]))
 
     far = other[kr]
     need("g", c_q)
-    put(far, T.ex[:, RX:RX + UN].bitcast(dt.uint8), T.cq[:, 0:UN].bitcast(dt.uint8), "rr")
-    put(far, T.exs[:, RX:RX + UN], T.cs[:, 0:UN], "rr")
+    put(far, T.ex[:, XR:XR + UN].bitcast(dt.uint8), T.cq[:, 0:UN].bitcast(dt.uint8), "rr")
+    put(far, T.exs[:, XR:XR + UN], T.cs[:, 0:UN], "rr")
 
-    need("v", po)
-    need("v", copy("v", T.ix[:, 0:2 * H].indirect(T.po[:, 0:4]), T.sv[:]))
-    need("v", did("v", V.tensor_tensor(T.ix[:], T.ix[:], T.uc[:], MUL)))
-    need("v", did("v", V.tensor_tensor(T.i2[:], T.ix[:, 0:2 * H:2], T.ix[:, 1:2 * H:2], ADD)))
-    need("v", did("v", V.tensor_tensor(T.i3[:], T.i2[:, 0:H:2], T.i2[:, 1:H:2], ADD)))
-    fo = did("v", V.tensor_scalar(T.fo[:], T.i3[:], 4.0, T.p3f[:, 0:1], op0=MUL, op1=ADD))
+    x = copy("v", T.ix[:, OC:NX], T.ix[:, 0:OC].indirect(T.pg[:, 2 * go:2 * go + 2]), ix)
+    need("v", place(go, UN, x))
+    need("v", did("v", V.tensor_tensor_scan(T.sc[:], T.ka[:], T.ix[:, 0:NX], 0.0, ADD, MAX)))
+    fo = did("v", V.tensor_scalar(T.fo[:], T.sc[:, 3:NX:4], 4.0, T.pc[:, 0:1], op0=MUL, op1=ADD))
 
-    for i in range(4):
-        need("t", lp[i])
-        own(i, 1, i, False)
     for s in (2, 1, 0):
         need("t", got("rl", s))
         for b in range(4):
-            last[b] = unpack(b, SEC * s + 2 * UN, b, False, s == 0)
-    wl = [copy("s", T.wl[:, b:128:4], ps(b, 96, 128), last[b]) for b in range(4)]
-    q = H // 4
-    gl = copy("s", T.gl[:], T.wl[:, 0:136].indirect(T.fo[:, q * gm:q * gm + OC // 4]), fo, c_all, *wl)
+            last[b] = unpack(b, xl(s), b, False, s == 0)
+    wl = [copy("s", T.tw[:, b:4 * UN:4], ps(b, 0, UN), last[b]) for b in range(4)]
+    al = copy("s", T.al[:], T.tw[:, 0:TR].indirect(T.fo[:, OC // 4:NX // 4]), c_all, fo, *wl)
 
     need("t", ("rr", 2 * len(topo.engines(far, core))))
-    rc = []
+    wr = []
     for b in range(4):
         need("t", cc[b])
-        rc.append(unpack(b, RX, 4 + b, True, True))
-    wr = [copy("v", T.wr[:, b:128:4], ps(4 + b, 0, UN), rc[b]) for b in range(4)]
-    need("v", fo, gl, *wr)
-    y = did("v", V.tensor_tensor(T.yt[:], T.wr[:, 0:136].indirect(T.fo[:, q * go:q * go + OC // 4]), T.gl[:], ADD))
-    need("y", y)
+        need("v", al, unpack(b, XR - 96, 4 + b, True, True))
+        wr.append(did("v", V.tensor_tensor(T.tw[:, TR + b:TR + 4 * UN:4], ps(4 + b, 96, 128), T.al[:, b:4 * UN:4], ADD)))
+    y = [copy(q, T.yt[:, 16 * lo:16 * hi], T.tw[:, 0:TR + 4 * UN].indirect(T.fo[:, lo:hi]), fo, *wr)
+         for q, lo, hi in (("v", 0, 8), ("s", 8, OC // 4))]
+    need("y", *y)
     SY.dma_start(T.y[:], T.yt[:]).then_inc(sem.st, 16)
     SY.wait_ge(sem.st, 16)
     g.wait_ge(sem.ls, sent[0])

@@ -1,8 +1,7 @@
-from concourse.bass import DstId, RemoteDMATransfer
 from concourse.mybir import dt, AluOpType, ActivationFunctionType
 
 UN, OC = 32, 56
-XL, XE, XS, XR = 0, 3 * UN, 3 * UN + 512, 6 * UN + 512
+XR, XL, XS, XE = 0, UN, 4 * UN, 7 * UN
 TR = 4 * (UN + 1)
 KEEP = 128
 NX = OC + UN
@@ -13,18 +12,16 @@ SCRATCH = {
     "aq": ("sbuf", [128, 512], "float8_e4m3fn_x4"),
     "asc": ("sbuf", [128, 512], "uint8"),
     "bw": ("sbuf", [128, 1024], "bfloat16"),
-    "bq": ("sbuf", [128, 256], "float8_e4m3fn_x4"),
-    "bsc": ("sbuf", [128, 256], "uint8"),
+    "bq": ("sbuf", [128, 384], "float8_e4m3fn_x4"),
+    "bsc": ("sbuf", [128, 384], "uint8"),
     "dn": ("sbuf", [128, 512], "bfloat16"),
     "dg": ("sbuf", [128, 516], "bfloat16"),
     "one": ("sbuf", [128, 128], "bfloat16"),
-    "ex": ("sbuf", [128, XR + UN], "float8_e4m3fn_x4"),
-    "exs": ("sbuf", [128, XR + UN], "uint8"),
-    "zt": ("sbuf", [128, 1024], "bfloat16"),
-    "zq": ("sbuf", [128, 256], "float8_e4m3fn_x4"),
-    "zs": ("sbuf", [128, 256], "uint8"),
-    "cq": ("sbuf", [128, 128], "float8_e4m3fn_x4"),
-    "cs": ("sbuf", [128, 128], "uint8"),
+    "ex": ("sbuf", [128, XE + 512], "float8_e4m3fn_x4"),
+    "exs": ("sbuf", [128, XE + 512], "uint8"),
+    "zt": ("sbuf", [128, 896], "bfloat16"),
+    "zq": ("sbuf", [128, 512], "float8_e4m3fn_x4"),
+    "zs": ("sbuf", [128, 512], "uint8"),
     "li": ("sbuf", [128, 16], "int32"),
     "lx": ("sbuf", [128, 16], "int32"),
     "base": ("sbuf", [128, 16], "int32"),
@@ -49,8 +46,8 @@ SCRATCH = {
     "yt": ("sbuf", [128, 4 * OC], "float32"),
     "ps": ("psum", [128, 4096], "float32"),
 }
-SEMAPHORES = ["v", "s", "t", "gp", "ldl", "ldb", "lda0", "lda1", "lda2", "ldu", "st", "ls",
-              "rc0", "rc1", "rc2", "rl0", "rl1", "rl2", "rr", "re"]
+SEMAPHORES = ["v", "s", "t", "gp", "ldl", "ldb", "lda0", "lda1", "lda2", "lda3", "ldu", "st", "ls",
+              "rc1", "rc2", "rc3", "rl1", "rl2", "rl3", "rr", "re"]
 
 ADD, SUB, MUL, AND, MIN, MAX, EQ = (AluOpType.add, AluOpType.subtract, AluOpType.mult, AluOpType.bitwise_and,
                                     AluOpType.min, AluOpType.max, AluOpType.is_equal)
@@ -75,7 +72,7 @@ def rank_program(g, core, T, topo):
 
     def need(qn, *ticks):
         q = {"v": V, "s": S, "t": PE, "g": g, "y": SY}[qn]
-        for name, n in ticks:
+        for name, n in dict(sorted(ticks)).items():
             if seen.get((qn, name), 0) < n:
                 seen[(qn, name)] = n
                 q.wait_ge(sem[name], n)
@@ -88,14 +85,19 @@ def rank_program(g, core, T, topo):
         return did("gp", g.iota(out, pattern, base, cm, allow_small_or_imprecise_dtypes=True) if fl
                    else g.iota(out, pattern, base, cm))
 
-    def put(dst_core, dst, src, name):
-        rid, pid = topo.addr(dst_core, core)
-        g.remote_dma(dst, src, sem[name], sem.ls, pid, rid, topo.mask(core, dst_core))
-        sent[0] += len(topo.engines(core, dst_core))
+    def quant(codes, scales, col, tile, *ticks):
+        need("v", *ticks)
+        return did("v", V.quantize_mx(codes[:, col:col + 128], scales[:, col:col + 128], tile))
 
-    def E(b):
-        o = XE + 128 * b
-        return T.ex[:, o:o + 128], T.exs[:, o:o + 128]
+    def put(to, col, n, codes, scales, at, name):
+        rid, pid = topo.addr(to, core)
+        for dst, src in ((T.ex[:, col:col + n].bitcast(dt.uint8), codes[:, at:at + n].bitcast(dt.uint8)),
+                         (T.exs[:, col:col + n], scales[:, at:at + n])):
+            g.remote_dma(dst, src, sem[name], sem.ls, pid, rid, topo.mask(core, to))
+            sent[0] += len(topo.engines(core, to))
+
+    def got(name, src):
+        return (name, 2 * len(topo.engines(src, core)))
 
     rank = T.rank_of(core)
     if rank is None:
@@ -103,10 +105,9 @@ def rank_program(g, core, T, topo):
         if served:
             did("v", V.memset(T.one[:], 1.0))
             need("g", did("v", V.memset(T.dg[:], 0.0)))
-            need("v", did("gp", g.affine_select(T.dg[:, 3:515:4], T.one[:], [[-1, 128]], EQ, 0.0, 0, 1)))
-            need("g", *[did("v", V.quantize_mx(*E(b), T.dg[:, 3 - b:3 - b + 512])) for b in range(4)])
-            put(served[0], T.ex[:, XE:XS].bitcast(dt.uint8), T.ex[:, XE:XS].bitcast(dt.uint8), "re")
-            put(served[0], T.exs[:, XE:XS], T.exs[:, XE:XS], "re")
+            diag = did("gp", g.affine_select(T.dg[:, 3:515:4], T.one[:], [[-1, 128]], EQ, 0.0, 0, 1))
+            need("g", *[quant(T.ex, T.exs, XE + 128 * b, T.dg[:, 3 - b:3 - b + 512], diag) for b in range(4)])
+            put(served[0], XE, 512, T.ex, T.exs, XE, "re")
             g.wait_ge(sem.ls, sent[0])
         return
 
@@ -117,30 +118,22 @@ def rank_program(g, core, T, topo):
     ho = T.rank_of(other[0])
     gm = 0 if topo.host(core) == topo.host(T.cores[0]) else 1
     go = 1 - gm
-    ka, kb = kr ^ 1, 2 - 2 * (kr // 2)
-    pos = {ka: 0, kb: 1, kb + 1: 2, kr: 3}
 
     for r in (0, 16):
         SY.dma_start(T.li[r:r + 16, 0:8], T.send[:]).then_inc(sem.ldl, 16)
         S.dma_start(T.li[r:r + 16, 8:16], T.un[:]).then_inc(sem.ldl, 16)
     S.dma_start(T.bt[:], T.b[:]).then_inc(sem.ldb, 16)
-    for k, (lo, hi) in enumerate(((0, 512), (512, 1536), (1536, 2048))):
-        SY.dma_start(T.at[:, lo:hi], T.a[:, lo:hi]).then_inc(sem["lda%d" % k], 16)
+    for i in range(4):
+        SY.dma_start(T.at[:, 512 * i:512 * i + 512], T.a[:, 512 * i:512 * i + 512]).then_inc(sem["lda%d" % i], 16)
     for r in range(0, 128, 16):
         SY.dma_start(T.up[r:r + 16, :], T.upl[:]).then_inc(sem.ldu, 16)
     LDL, LDB, LDU = ("ldl", 64), ("ldb", 16), ("ldu", 128)
 
-    z_base = did("v", V.memset(T.base[:], 0))
+    did("v", V.memset(T.base[:, 0:8], 0))
     z_bw = did("v", V.memset(T.bw[:, 0:512], 0.0))
-    did("v", V.memset(T.zt[:, 512:640], 0.0))
+    did("v", V.memset(T.zt[:, 128:512], 0.0))
+    b_base = iota(T.base[:, 8:16], [[0, 2], [UN - 2 * UN * (kr % 2), 2], [0, 2]], UN * (kr % 2))
     p_idx = iota(T.pidx[:], [[0, 4]], 0, 1 + KEEP)
-    need("g", z_base)
-    c = 8 + ho + 2 * (kb + 1)
-    b_base = iota(T.base[:, c:c + 1], [[0, 1]], UN)
-    if kr < 3:
-        b_base = iota(T.base[:, 8 + hm + 2 * (kr + 1):16:2], [[UN, 3 - kr]], UN)
-    if kr > 0:
-        b_base = iota(T.base[:, 8 + hm:8 + hm + 2 * kr:2], [[UN, kr]], UN * (4 - kr))
     iota(T.kc[:], [[1, 4]], NX, 4)
     iota(T.ka[:], [[0, NX // 4], [8 * KEEP, 4]], 0, 0, True)
     iota(T.sv[:], [[UN + 1, 2], [1, UN]], 0, 0, True)
@@ -160,32 +153,28 @@ def rank_program(g, core, T, topo):
     def offsets(out, h):
         return [did("v", V.tensor_scalar(out[:, t:32:4], T.lx[:, h:16:2], 4, t, op0=MUL, op1=ADD)) for t in range(4)][3]
 
-    oc = offsets(T.oc, ho)
-    pieces = [(ka, 1), (kb, 2), (kr, 1)]
-    dn_c = [copy("s", T.dn[:, 64 * pos[k]:64 * (pos[k] + n)], T.bt[:, 0:512].indirect(T.oc[:, 4 * k:4 * (k + n)]), LDB, oc)
-            for k, n in pieces]
-    ol = offsets(T.ol, hm)
-    dn_l = copy("s", T.dn[:, 256:512], T.bt[:, 0:512].indirect(T.ol[:, 0:16]), ol)
+    off = [(T.oc, offsets(T.oc, ho)), (T.ol, offsets(T.ol, hm))]
+    dn = {}
 
-    def scatter(u):
-        k, n = pieces[u]
-        return copy("v", T.bw[:, 128 * pos[k]:128 * (pos[k] + n)].indirect(T.oc[:, 16 + 4 * k:16 + 4 * (k + n)]),
-                    T.dn[:, 64 * pos[k]:64 * (pos[k] + n)], oc, dn_c[u])
+    def span(half, js):
+        k = min(j ^ kr for j in js)
+        return k, T.dn[:, 256 * half + 64 * k:256 * half + 64 * (k + len(js))]
 
-    def quant_b(half, *ticks):
-        need("v", *ticks)
-        lo = 128 * half
-        return did("v", V.quantize_mx(T.bq[:, lo:lo + 128], T.bsc[:, lo:lo + 128], T.bw[:, 4 * lo:4 * lo + 512]))
+    for half, js in ((0, (1,)), (0, (2, 3)), (0, (0,)), (1, (2, 3)), (1, (1,)), (1, (0,))):
+        k, d = span(half, js)
+        dn[half, js] = copy("s", d, T.bt[:, 0:512].indirect(off[half][0][:, 4 * k:4 * (k + len(js))]), LDB, off[half][1])
+
+    def scatter(half, js, *ticks):
+        k, d = span(half, js)
+        lo = 512 * half + 256 * (js[0] // 2)
+        return copy("v", T.bw[:, lo:lo + 256].indirect(off[half][0][:, 16 + 4 * k:16 + 4 * (k + len(js))]), d,
+                    off[half][1], dn[half, js], *ticks)
+
+    def quant_b(half, to, *ticks):
+        return quant(T.bq, T.bsc, 128 * to, T.bw[:, 512 * half:512 * half + 512], *ticks)
 
     def quant_a(i):
-        need("v", ("lda%d" % ((i + 1) // 2), 16))
-        return did("v", V.quantize_mx(T.aq[:, 128 * i:128 * i + 128], T.asc[:, 128 * i:128 * i + 128],
-                                      T.at[:, 512 * i:512 * i + 512]))
-
-    x = [scatter(0), scatter(1)]
-    a_q = [quant_a(0)]
-    b_c = quant_b(0, *x)
-    a_q += [quant_a(i) for i in (1, 2, 3)]
+        return quant(T.aq, T.asc, 128 * i, T.at[:, 512 * i:512 * i + 512], ("lda%d" % i, 16))
 
     def own(i, half, bank, stop, *ticks):
         need("t", a_q[i], *ticks)
@@ -195,101 +184,89 @@ def rank_program(g, core, T, topo):
                                      True, stop))
 
     def unpack(b, col, bank, start, stop):
-        c, s = E(b)
-        need("t", ("re", 2 * len(topo.engines(helper_of(core, topo), core))))
-        return did("t", PE.matmul_mx(T.ps[:, 512 * bank:512 * bank + 128], c, s,
+        e = XE + 128 * b
+        need("t", got("re", helper_of(core, topo)))
+        return did("t", PE.matmul_mx(T.ps[:, 512 * bank:512 * bank + 128], T.ex[:, e:e + 128], T.exs[:, e:e + 128],
                                      T.ex[:, col:col + 128], T.exs[:, col:col + 128], start, stop))
 
     def ps(bank, lo, hi):
         return T.ps[:, 512 * bank + lo:512 * bank + hi]
 
-    zc = [own(i, 0, i, True, b_c) for i in range(4)]
-    cp = [copy("s", T.zt[:, 128 + i:512:4], ps(i, 0, 96), zc[i]) for i in range(4)]
-    need("v", b_c)
-    s_own = scatter(2)
-    need("v", *cp)
-    zq_c = did("v", V.quantize_mx(T.zq[:, 0:128], T.zs[:, 0:128], T.zt[:, 128:640]))
+    def hop1(name, x0, at, j):
+        put(mine[kr ^ j], x0 + UN * (3 - j), UN, T.zq, T.zs, at, name + str(j))
 
-    peers = [mine[(kr + 1 + j) % 4] for j in range(3)]
-
-    def hop1(name, col, at):
-        for j in range(3):
-            o, c = at(2 - j), col(j)
-            put(peers[j], T.ex[:, o:o + UN].bitcast(dt.uint8), T.zq[:, c:c + UN].bitcast(dt.uint8), name + str(2 - j))
-            put(peers[j], T.exs[:, o:o + UN], T.zs[:, c:c + UN], name + str(2 - j))
-
-    def got(name, s):
-        return (name + str(s), 2 * len(topo.engines(mine[(kr + 1 + s) % 4], core)))
-
-    def xs(s):
-        return XS + UN * (2 - s)
-
-    def xl(s):
-        return XL + UN * s
-
-    need("g", zq_c)
-    hop1("rc", lambda j: UN * pos[(kr + 1 + j) % 4], xs)
-
-    b_own = quant_b(0, s_own)
-    for i in range(4):
-        own(i, 0, 4 + i, False, b_own)
-
-    b_l = quant_b(1, copy("v", T.bw[:, 512:1024].indirect(T.ol[:, 16:32]), T.dn[:, 256:512], ol, dn_l))
-    zl = [own(i, 1, i, True, b_l, cp[i]) for i in range(4)]
-    lp = [copy("s", T.zt[:, 640 + i:1024:4], ps(i, UN, 128), zl[i]) for i in range(4)]
-    for i in range(4):
-        own(i, 1, i, False, lp[i])
-
+    a_q = [quant_a(0), quant_a(1)]
+    x = scatter(0, (1,))
+    a_q += [quant_a(2)]
+    b_1 = quant_b(0, 0, x)
+    a_q += [quant_a(3)]
+    cp = [copy("s", T.zt[:, i:128:4], ps(i, UN, 2 * UN), own(i, 0, i, True, b_1)) for i in range(4)]
+    s_2 = scatter(0, (2, 3), b_1)
     need("v", LDU, c_all)
-    x = did("v", V.tensor_scalar(T.um[:], T.up[:], 1023, None, op0=AND))
-    did("v", V.tensor_scalar(T.ka[:], T.ka[:], T.pa[:, 0:1], KEEP, op0=SUB, op1=MIN))
-    need("v", x)
-    x = did("v", V.tensor_tensor(T.um[:], T.um[:], T.kc[:], MIN))
+    um = did("v", V.tensor_scalar(T.um[:], T.up[:], 1023, None, op0=AND))
     copy("v", T.pg[:], T.up[:])
-    x = copy("v", T.po[:], T.um[:], x)
+    b_2 = quant_b(0, 2, s_2)
+    zq_1 = quant(T.zq, T.zs, 0, T.zt[:, 0:512], *cp)
+    need("g", zq_1)
+    hop1("rc", XS, 0, 1)
+
+    cp = [copy("s", T.zt[:, 128 + i:384:4], ps(i, 2 * UN, 128), own(i, 2, i, True, b_2, cp[i]), zq_1) for i in range(4)]
+    s_l = [scatter(1, (2, 3)), scatter(1, (1,))]
+    zq_2 = quant(T.zq, T.zs, 128, T.zt[:, 0:512], *cp)
+    need("g", zq_2)
+    for j in (2, 3):
+        hop1("rc", XS, 128 + UN * (j - 1), j)
+    b_l = quant_b(1, 1, *s_l)
+    lp = [copy("s", T.zt[:, 512 + i:896:4], ps(i, UN, 128), own(i, 1, i, True, b_l, cp[i])) for i in range(4)]
+
+    s_own = scatter(0, (0,))
+    did("v", V.tensor_scalar(T.ka[:], T.ka[:], T.pa[:, 0:1], KEEP, op0=SUB, op1=MIN))
+    need("v", um)
+    um = did("v", V.tensor_tensor(T.um[:], T.um[:], T.kc[:], MIN))
+    x = quant_b(0, 0, s_own)
+    for i in range(4):
+        own(i, 0, 4 + i, False, x)
 
     def place(h, lo, *ticks):
         return copy("v", T.ix[:, 0:NX + 512].indirect(T.po[:, 2 * h:2 * h + 2]), T.sv[:, lo:lo + UN], *ticks)
 
-    ix = place(gm, 0, x)
-
-    need("v", *lp)
-    zq_l = did("v", V.quantize_mx(T.zq[:, 128:256], T.zs[:, 128:256], T.zt[:, 512:1024]))
+    po = copy("v", T.po[:], T.um[:], um)
+    s_own = scatter(1, (0,), b_l)
+    x = place(gm, 0, po)
+    zq_l = quant(T.zq, T.zs, 256, T.zt[:, 384:896], *lp)
     need("g", zq_l)
-    hop1("rl", lambda j: 128 + UN * (j + 1), xl)
-
-    last = [None] * 4
-    for s in (2, 1, 0):
-        need("t", got("rc", s))
-        for b in range(4):
-            last[b] = unpack(b, xs(s) - 96, 4 + b, False, s == 0)
-    cc = [copy("svsv"[b], T.zt[:, b:128:4], ps(4 + b, 96, 128), last[b]) for b in range(4)]
-    need("v", *cc)
-    c_q = did("v", V.quantize_mx(T.cq[:], T.cs[:], T.zt[:, 0:512]))
-
-    far = other[kr]
-    need("g", c_q)
-    put(far, T.ex[:, XR:XR + UN].bitcast(dt.uint8), T.cq[:, 0:UN].bitcast(dt.uint8), "rr")
-    put(far, T.exs[:, XR:XR + UN], T.cs[:, 0:UN], "rr")
-
-    x = copy("v", T.ix[:, OC:NX], T.ix[:, 0:OC].indirect(T.pg[:, 2 * go:2 * go + 2]), ix)
+    for j in (1, 2, 3):
+        hop1("rl", XL, 256 + UN * j, j)
+    x = copy("v", T.ix[:, OC:NX], T.ix[:, 0:OC].indirect(T.pg[:, 2 * go:2 * go + 2]), x)
+    b_own = quant_b(1, 1, s_own)
     need("v", place(go, UN, x))
     need("v", did("v", V.tensor_tensor_scan(T.sc[:], T.ka[:], T.ix[:, 0:NX], 0.0, ADD, MAX)))
     fo = did("v", V.tensor_scalar(T.fo[:], T.sc[:, 3:NX:4], 4.0, T.pc[:, 0:1], op0=MUL, op1=ADD))
 
-    for s in (2, 1, 0):
-        need("t", got("rl", s))
-        for b in range(4):
-            last[b] = unpack(b, xl(s), b, False, s == 0)
+    def add_up(name, x0, bank):
+        for j in (1, 2, 3):
+            need("t", got(name + str(j), mine[kr ^ j]))
+            last = [unpack(b, x0 + UN * (3 - j), bank + b, False, j == 3) for b in range(4)]
+        return last
+
+    last = add_up("rc", XS, 4)
+    cc = [copy("svsv"[b], T.zt[:, 384 + b:512:4], ps(4 + b, 0, UN), last[b], zq_l) for b in range(4)]
+    need("g", quant(T.zq, T.zs, 384, T.zt[:, 384:896], *cc))
+    far = other[kr]
+    put(far, XR, UN, T.zq, T.zs, 384, "rr")
+
+    for i in range(4):
+        own(i, 1, i, False, b_own)
+    last = add_up("rl", XL, 0)
     wl = [copy("s", T.tw[:, b:4 * UN:4], ps(b, 0, UN), last[b]) for b in range(4)]
     al = copy("s", T.al[:], T.tw[:, 0:TR].indirect(T.fo[:, OC // 4:NX // 4]), c_all, fo, *wl)
 
-    need("t", ("rr", 2 * len(topo.engines(far, core))))
+    need("t", got("rr", far))
     wr = []
     for b in range(4):
         need("t", cc[b])
-        need("v", al, unpack(b, XR - 96, 4 + b, True, True))
-        wr.append(did("v", V.tensor_tensor(T.tw[:, TR + b:TR + 4 * UN:4], ps(4 + b, 96, 128), T.al[:, b:4 * UN:4], ADD)))
+        need("v", al, unpack(b, XR, 4 + b, True, True))
+        wr.append(did("v", V.tensor_tensor(T.tw[:, TR + b:TR + 4 * UN:4], ps(4 + b, 0, UN), T.al[:, b:4 * UN:4], ADD)))
     y = [copy(q, T.yt[:, 16 * lo:16 * hi], T.tw[:, 0:TR + 4 * UN].indirect(T.fo[:, lo:hi]), fo, *wr)
          for q, lo, hi in (("v", 0, 8), ("s", 8, OC // 4))]
     need("y", *y)

from concourse.mybir import dt, AluOpType, ActivationFunctionType

UN, OC = 32, 56
XR, XL, XS, XE = 0, UN, 4 * UN, 7 * UN
TR = 4 * (UN + 1)
KEEP = 128
NX = OC + UN

SCRATCH = {
    "at": ("sbuf", [128, 2048], "bfloat16"),
    "bt": ("sbuf", [128, 512], "bfloat16"),
    "aq": ("sbuf", [128, 512], "float8_e4m3fn_x4"),
    "asc": ("sbuf", [128, 512], "uint8"),
    "bw": ("sbuf", [128, 1024], "bfloat16"),
    "bq": ("sbuf", [128, 384], "float8_e4m3fn_x4"),
    "bsc": ("sbuf", [128, 384], "uint8"),
    "dn": ("sbuf", [128, 512], "bfloat16"),
    "dg": ("sbuf", [128, 516], "bfloat16"),
    "one": ("sbuf", [128, 128], "bfloat16"),
    "ex": ("sbuf", [128, XE + 512], "float8_e4m3fn_x4"),
    "exs": ("sbuf", [128, XE + 512], "uint8"),
    "zt": ("sbuf", [128, 896], "bfloat16"),
    "zq": ("sbuf", [128, 512], "float8_e4m3fn_x4"),
    "zs": ("sbuf", [128, 512], "uint8"),
    "li": ("sbuf", [128, 16], "int32"),
    "lx": ("sbuf", [128, 16], "int32"),
    "base": ("sbuf", [128, 16], "int32"),
    "oc": ("sbuf", [128, 32], "uint16"),
    "ol": ("sbuf", [128, 32], "uint16"),
    "up": ("sbuf", [128, 4], "int32"),
    "um": ("sbuf", [128, 4], "int32"),
    "kc": ("sbuf", [128, 4], "int32"),
    "po": ("sbuf", [128, 4], "uint16"),
    "pg": ("sbuf", [128, 4], "uint16"),
    "pidx": ("sbuf", [128, 4], "int32"),
    "pm": ("sbuf", [128, 4], "int32"),
    "pa": ("sbuf", [128, 4], "float32"),
    "pc": ("sbuf", [128, 4], "float32"),
    "sv": ("sbuf", [128, 2 * UN], "float32"),
    "ka": ("sbuf", [128, NX], "float32"),
    "ix": ("sbuf", [128, NX + 512], "float32"),
    "sc": ("sbuf", [128, NX], "float32"),
    "fo": ("sbuf", [128, NX // 4], "uint16"),
    "tw": ("sbuf", [128, TR + 4 * UN], "float32"),
    "al": ("sbuf", [128, 4 * UN], "float32"),
    "yt": ("sbuf", [128, 4 * OC], "float32"),
    "ps": ("psum", [128, 4096], "float32"),
}
SEMAPHORES = ["v", "s", "t", "gp", "ldl", "ldb", "lda0", "lda1", "lda2", "lda3", "ldu", "st", "ls",
              "rc1", "rc2", "rc3", "rl1", "rl2", "rl3", "rr", "re"]

ADD, SUB, MUL, AND, MIN, MAX, EQ = (AluOpType.add, AluOpType.subtract, AluOpType.mult, AluOpType.bitwise_and,
                                    AluOpType.min, AluOpType.max, AluOpType.is_equal)
COPY = ActivationFunctionType.Copy


def helper_of(core, topo):
    return [c for c in topo.cores_of(core) if c != core and topo.die(c) == topo.die(core)][0]


def rank_program(g, core, T, topo):
    V, S, PE, SY = g.vector, g.scalar, g.tensor, g.sync
    sem = T.sem
    tick = {"v": 0, "s": 0, "t": 0, "gp": 0}
    seen = {}
    sent = [0]

    def did(name, ins):
        ins.then_inc(sem[name], 1)
        tick[name] += 1
        return (name, tick[name])

    def need(qn, *ticks):
        q = {"v": V, "s": S, "t": PE, "g": g, "y": SY}[qn]
        for name, n in dict(sorted(ticks)).items():
            if seen.get((qn, name), 0) < n:
                seen[(qn, name)] = n
                q.wait_ge(sem[name], n)

    def copy(qn, out, in_, *ticks):
        need(qn, *ticks)
        return did(qn, S.activation(out, in_, COPY) if qn == "s" else V.tensor_copy(out, in_))

    def iota(out, pattern, base, cm=0, fl=False):
        return did("gp", g.iota(out, pattern, base, cm, allow_small_or_imprecise_dtypes=True) if fl
                   else g.iota(out, pattern, base, cm))

    def quant(codes, scales, col, tile, *ticks):
        need("v", *ticks)
        return did("v", V.quantize_mx(codes[:, col:col + 128], scales[:, col:col + 128], tile))

    def put(to, col, n, codes, scales, at, name):
        rid, pid = topo.addr(to, core)
        for dst, src in ((T.ex[:, col:col + n].bitcast(dt.uint8), codes[:, at:at + n].bitcast(dt.uint8)),
                         (T.exs[:, col:col + n], scales[:, at:at + n])):
            g.remote_dma(dst, src, sem[name], sem.ls, pid, rid, topo.mask(core, to))
            sent[0] += len(topo.engines(core, to))

    def got(name, src):
        return (name, 2 * len(topo.engines(src, core)))

    rank = T.rank_of(core)
    if rank is None:
        served = [c for c in T.cores if helper_of(c, topo) == core]
        if served:
            did("v", V.memset(T.one[:], 1.0))
            need("g", did("v", V.memset(T.dg[:], 0.0)))
            diag = did("gp", g.affine_select(T.dg[:, 3:515:4], T.one[:], [[-1, 128]], EQ, 0.0, 0, 1))
            need("g", *[quant(T.ex, T.exs, XE + 128 * b, T.dg[:, 3 - b:3 - b + 512], diag) for b in range(4)])
            put(served[0], XE, 512, T.ex, T.exs, XE, "re")
            g.wait_ge(sem.ls, sent[0])
        return

    mine = [c for c in T.cores if topo.host(c) == topo.host(core)]
    other = [c for c in T.cores if topo.host(c) != topo.host(core)]
    kr = mine.index(core)
    hm = T.rank_of(mine[0])
    ho = T.rank_of(other[0])
    gm = 0 if topo.host(core) == topo.host(T.cores[0]) else 1
    go = 1 - gm

    for r in (0, 16):
        SY.dma_start(T.li[r:r + 16, 0:8], T.send[:]).then_inc(sem.ldl, 16)
        S.dma_start(T.li[r:r + 16, 8:16], T.un[:]).then_inc(sem.ldl, 16)
    S.dma_start(T.bt[:], T.b[:]).then_inc(sem.ldb, 16)
    for i in range(4):
        SY.dma_start(T.at[:, 512 * i:512 * i + 512], T.a[:, 512 * i:512 * i + 512]).then_inc(sem["lda%d" % i], 16)
    for r in range(0, 128, 16):
        SY.dma_start(T.up[r:r + 16, :], T.upl[:]).then_inc(sem.ldu, 16)
    LDL, LDB, LDU = ("ldl", 64), ("ldb", 16), ("ldu", 128)

    did("v", V.memset(T.base[:, 0:8], 0))
    z_bw = did("v", V.memset(T.bw[:, 0:512], 0.0))
    did("v", V.memset(T.zt[:, 128:512], 0.0))
    b_base = iota(T.base[:, 8:16], [[0, 2], [UN - 2 * UN * (kr % 2), 2], [0, 2]], UN * (kr % 2))
    p_idx = iota(T.pidx[:], [[0, 4]], 0, 1 + KEEP)
    iota(T.kc[:], [[1, 4]], NX, 4)
    iota(T.ka[:], [[0, NX // 4], [8 * KEEP, 4]], 0, 0, True)
    iota(T.sv[:], [[UN + 1, 2], [1, UN]], 0, 0, True)
    iota(T.ix[:, 0:OC], [[0, OC]], UN, 0, True)
    c_all = iota(T.tw[:, 4 * UN:TR], [[0, 4]], 0, 0, True)
    copy("s", T.bw[:, 512:1024], T.bw[:, 0:512], z_bw)
    need("v", p_idx)
    need("v", did("v", V.tensor_scalar(T.pm[:], T.pidx[:], 3 + 12 * KEEP, None, op0=AND)))
    did("v", V.tensor_scalar(T.pa[:], T.pm[:], 2, 4 * KEEP, op0=MUL, op1=ADD))
    did("v", V.tensor_scalar(T.pc[:], T.pm[:], -12 * KEEP, None, op0=ADD))

    need("v", LDL, b_base)
    for r in range(0, 128, 32):
        x = did("v", V.tensor_tensor(T.lx[r:r + 32, :], T.li[0:32, :], T.base[0:32, :], ADD))
    need("v", x)

    def offsets(out, h):
        return [did("v", V.tensor_scalar(out[:, t:32:4], T.lx[:, h:16:2], 4, t, op0=MUL, op1=ADD)) for t in range(4)][3]

    off = [(T.oc, offsets(T.oc, ho)), (T.ol, offsets(T.ol, hm))]
    dn = {}

    def span(half, js):
        k = min(j ^ kr for j in js)
        return k, T.dn[:, 256 * half + 64 * k:256 * half + 64 * (k + len(js))]

    for half, js in ((0, (1,)), (0, (2, 3)), (0, (0,)), (1, (2, 3)), (1, (1,)), (1, (0,))):
        k, d = span(half, js)
        dn[half, js] = copy("s", d, T.bt[:, 0:512].indirect(off[half][0][:, 4 * k:4 * (k + len(js))]), LDB, off[half][1])

    def scatter(half, js, *ticks):
        k, d = span(half, js)
        lo = 512 * half + 256 * (js[0] // 2)
        return copy("v", T.bw[:, lo:lo + 256].indirect(off[half][0][:, 16 + 4 * k:16 + 4 * (k + len(js))]), d,
                    off[half][1], dn[half, js], *ticks)

    def quant_b(half, to, *ticks):
        return quant(T.bq, T.bsc, 128 * to, T.bw[:, 512 * half:512 * half + 512], *ticks)

    def quant_a(i):
        return quant(T.aq, T.asc, 128 * i, T.at[:, 512 * i:512 * i + 512], ("lda%d" % i, 16))

    def own(i, half, bank, stop, *ticks):
        need("t", a_q[i], *ticks)
        return did("t", PE.matmul_mx(T.ps[:, 512 * bank:512 * bank + 128],
                                     T.aq[:, 128 * i:128 * i + 128], T.asc[:, 128 * i:128 * i + 128],
                                     T.bq[:, 128 * half:128 * half + 128], T.bsc[:, 128 * half:128 * half + 128],
                                     True, stop))

    def unpack(b, col, bank, start, stop):
        e = XE + 128 * b
        need("t", got("re", helper_of(core, topo)))
        return did("t", PE.matmul_mx(T.ps[:, 512 * bank:512 * bank + 128], T.ex[:, e:e + 128], T.exs[:, e:e + 128],
                                     T.ex[:, col:col + 128], T.exs[:, col:col + 128], start, stop))

    def ps(bank, lo, hi):
        return T.ps[:, 512 * bank + lo:512 * bank + hi]

    def hop1(name, x0, at, j):
        put(mine[kr ^ j], x0 + UN * (3 - j), UN, T.zq, T.zs, at, name + str(j))

    a_q = [quant_a(0), quant_a(1)]
    x = scatter(0, (1,))
    a_q += [quant_a(2)]
    b_1 = quant_b(0, 0, x)
    a_q += [quant_a(3)]
    cp = [copy("s", T.zt[:, i:128:4], ps(i, UN, 2 * UN), own(i, 0, i, True, b_1)) for i in range(4)]
    s_2 = scatter(0, (2, 3), b_1)
    need("v", LDU, c_all)
    um = did("v", V.tensor_scalar(T.um[:], T.up[:], 1023, None, op0=AND))
    copy("v", T.pg[:], T.up[:])
    b_2 = quant_b(0, 2, s_2)
    zq_1 = quant(T.zq, T.zs, 0, T.zt[:, 0:512], *cp)
    need("g", zq_1)
    hop1("rc", XS, 0, 1)

    cp = [copy("s", T.zt[:, 128 + i:384:4], ps(i, 2 * UN, 128), own(i, 2, i, True, b_2, cp[i]), zq_1) for i in range(4)]
    s_l = [scatter(1, (2, 3)), scatter(1, (1,))]
    zq_2 = quant(T.zq, T.zs, 128, T.zt[:, 0:512], *cp)
    need("g", zq_2)
    for j in (2, 3):
        hop1("rc", XS, 128 + UN * (j - 1), j)
    b_l = quant_b(1, 1, *s_l)
    lp = [copy("s", T.zt[:, 512 + i:896:4], ps(i, UN, 128), own(i, 1, i, True, b_l, cp[i])) for i in range(4)]

    s_own = scatter(0, (0,))
    did("v", V.tensor_scalar(T.ka[:], T.ka[:], T.pa[:, 0:1], KEEP, op0=SUB, op1=MIN))
    need("v", um)
    um = did("v", V.tensor_tensor(T.um[:], T.um[:], T.kc[:], MIN))
    x = quant_b(0, 0, s_own)
    for i in range(4):
        own(i, 0, 4 + i, False, x)

    def place(h, lo, *ticks):
        return copy("v", T.ix[:, 0:NX + 512].indirect(T.po[:, 2 * h:2 * h + 2]), T.sv[:, lo:lo + UN], *ticks)

    po = copy("v", T.po[:], T.um[:], um)
    s_own = scatter(1, (0,), b_l)
    x = place(gm, 0, po)
    zq_l = quant(T.zq, T.zs, 256, T.zt[:, 384:896], *lp)
    need("g", zq_l)
    for j in (1, 2, 3):
        hop1("rl", XL, 256 + UN * j, j)
    x = copy("v", T.ix[:, OC:NX], T.ix[:, 0:OC].indirect(T.pg[:, 2 * go:2 * go + 2]), x)
    b_own = quant_b(1, 1, s_own)
    need("v", place(go, UN, x))
    need("v", did("v", V.tensor_tensor_scan(T.sc[:], T.ka[:], T.ix[:, 0:NX], 0.0, ADD, MAX)))
    fo = did("v", V.tensor_scalar(T.fo[:], T.sc[:, 3:NX:4], 4.0, T.pc[:, 0:1], op0=MUL, op1=ADD))

    def add_up(name, x0, bank):
        for j in (1, 2, 3):
            need("t", got(name + str(j), mine[kr ^ j]))
            last = [unpack(b, x0 + UN * (3 - j), bank + b, False, j == 3) for b in range(4)]
        return last

    last = add_up("rc", XS, 4)
    cc = [copy("svsv"[b], T.zt[:, 384 + b:512:4], ps(4 + b, 0, UN), last[b], zq_l) for b in range(4)]
    need("g", quant(T.zq, T.zs, 384, T.zt[:, 384:896], *cc))
    far = other[kr]
    put(far, XR, UN, T.zq, T.zs, 384, "rr")

    for i in range(4):
        own(i, 1, i, False, b_own)
    last = add_up("rl", XL, 0)
    wl = [copy("s", T.tw[:, b:4 * UN:4], ps(b, 0, UN), last[b]) for b in range(4)]
    al = copy("s", T.al[:], T.tw[:, 0:TR].indirect(T.fo[:, OC // 4:NX // 4]), c_all, fo, *wl)

    need("t", got("rr", far))
    wr = []
    for b in range(4):
        need("t", cc[b])
        need("v", al, unpack(b, XR, 4 + b, True, True))
        wr.append(did("v", V.tensor_tensor(T.tw[:, TR + b:TR + 4 * UN:4], ps(4 + b, 0, UN), T.al[:, b:4 * UN:4], ADD)))
    y = [copy(q, T.yt[:, 16 * lo:16 * hi], T.tw[:, 0:TR + 4 * UN].indirect(T.fo[:, lo:hi]), fo, *wr)
         for q, lo, hi in (("v", 0, 8), ("s", 8, OC // 4))]
    need("y", *y)
    SY.dma_start(T.y[:], T.yt[:]).then_inc(sem.st, 16)
    SY.wait_ge(sem.st, 16)
    g.wait_ge(sem.ls, sent[0])
    need("g", ("v", tick["v"]), ("s", tick["s"]), ("t", tick["t"]))
